import numpy as np
import ml_dtypes


def mxq(x, axis, fmt="e4m3"):
    dtype, down = {"e4m3": (ml_dtypes.float8_e4m3fn, 7), "e5m2": (ml_dtypes.float8_e5m2, 14)}[fmt]
    v = np.moveaxis(np.asarray(x, np.float32).astype(ml_dtypes.bfloat16).astype(np.float64), axis, -1)
    blocks = v.reshape(v.shape[:-1] + (-1, 32))
    amax = np.abs(blocks).max(-1, keepdims=True)
    byte = np.maximum(np.where(amax > 0, np.frexp(amax)[1] - 1 + 127, 0) - down, 1)
    scale = np.exp2(byte - 127.0)
    codes = (blocks / scale).astype(np.float32).astype(dtype).astype(np.float64)
    return np.moveaxis((codes * scale).reshape(v.shape), -1, axis)


WIDE = False


def mx_kscale(k):
    if not WIDE:
        return np.ones(k)
    levels = np.array([10, -10, 5, -5, 0])
    if k % 512:
        return np.exp2(np.random.permutation(np.resize(levels, k // 32))).repeat(32)
    a = np.empty((k // 512, 16))
    for p in range(k // 512):
        a[p, :8] = np.random.permutation(np.resize(levels, 8))
        for g in range(8):
            far = levels[np.abs(levels - a[p, g]) >= 10]
            a[p, g + 8] = far[np.random.randint(len(far))]
    return np.exp2(a.ravel()).repeat(32)


def f64(x):
    return np.asarray(x).astype(np.float64)


def striped(idx):
    return np.tile(idx.reshape(-1, 16).T, (8, 1)).astype(np.uint16)


def unstriped(offs):
    return offs[:16].T.reshape(-1).astype(np.int64)


def pack_weight(w):
    k, n = w.shape
    w = f64(np.asarray(w, np.float32).astype(ml_dtypes.bfloat16)).reshape(k // 32, 32, n)
    amax = np.abs(w).max(1)
    byte = np.clip(np.where(amax > 0, np.frexp(amax)[1] - 1 + 127 - 7, 1), 1, 254)
    scaled = (w * np.exp2(127.0 - byte)[:, None, :]).reshape(k, n).astype(np.float32)
    words = np.ascontiguousarray(scaled.reshape(k // 512, 128, 4, n).transpose(0, 1, 3, 2)).astype(ml_dtypes.float8_e4m3fn).view(np.uint8)
    return words, np.ascontiguousarray(byte.astype(np.uint8).reshape(k // 512, 16, n))


def unpack_weight(words, scales):
    g, p, n, _ = words.shape
    vals = np.ascontiguousarray(words).view(ml_dtypes.float8_e4m3fn).astype(np.float64) * np.repeat(np.exp2(scales.astype(np.float64) - 127.0), 8, axis=1)[..., None]
    return vals.transpose(0, 1, 3, 2).reshape(g * 512, n)


K, T, S, D, N, V = 1024, 4096, 1024, 8, 128, 128
P = 2 ** 7


def setup_inputs():
    n = np.random.standard_normal
    s = mx_kscale(K)[:, None]
    packed_xT = pack_weight(n((K, T)) * s)
    return {
        "x_words": packed_xT[0],
        "x_scales": packed_xT[1],
        "w1": (n((K, N)) / np.sqrt(K) / s).astype(np.float32),
        "bin_": (np.tile(np.tile(np.arange(D), V), (P, 1))).astype(np.float32),
        "offs": striped(np.random.permutation(T)[:S]),
    }


def reference(x_words, x_scales, w1, bin_, offs):
    xq = unpack_weight(x_words, x_scales)[:, unstriped(offs)]
    y = mxq(f64(w1), 0, "e4m3").T @ xq
    top = y.reshape(len(y), -1, D).max(axis=2)
    ex = np.exp(y - np.repeat(top, D, axis=1))
    tot = ex.reshape(len(ex), -1, D).sum(axis=2)
    pr = ex / np.repeat(tot, D, axis=1)
    pb = pr * f64(bin_)[:1]
    ed = pb.reshape(len(pb), -1, D).sum(axis=2)
    pv = pr * ((f64(bin_)[:1] - np.repeat(ed, D, axis=1)) ** 2)
    return ed + 0.5 * (np.sqrt(pv.reshape(len(pv), -1, D).sum(axis=2) + 0.05))

@@ -1,0 +1,165 @@
+from contextlib import ExitStack
+
+import concourse.mybir as mybir
+from concourse.masks import make_identity
+
+K, T, S, D, M = 1024, 4096, 1024, 8, 128
+V = S // D
+FLOPS = 2 * K * M * S
+
+F32 = mybir.dt.float32
+BF16 = mybir.dt.bfloat16
+I32 = mybir.dt.int32
+U32 = mybir.dt.uint32
+U16 = mybir.dt.uint16
+U8 = mybir.dt.uint8
+FP8X4 = mybir.dt.float8_e4m3fn_x4
+ALU = mybir.AluOpType
+ACT = mybir.ActivationFunctionType
+AX = mybir.AxisListType
+
+P = 128
+PASSES = 2
+HALF = S // 2
+VH = V // 2
+DG = D // 2
+
+
+def tile_picked_ydfl_dist_p_kernel(tc, x_words, x_scales, w1, bin_, offs, out):
+    nc = tc.nc
+    with ExitStack() as ctx:
+        keep = ctx.enter_context(tc.tile_pool(name="keep", bufs=1))
+        psum = ctx.enter_context(tc.psum_pool(name="psum", bufs=1))
+
+        offsets = keep.tile([P, S // 16], U16, name="offsets")
+        nc.sync.dma_start(offsets[:], offs)
+
+        scale_table = keep.tile([P, T], U8, name="scale_table", align_bytes=64)
+        nc.sync.dma_start(
+            scale_table[0:32, :].bitcast(I32),
+            x_scales.rearrange("o q c -> (o q) c").bitcast(I32),
+        )
+        nc.vector.memset(scale_table[32:64, :].bitcast(I32), 0)
+        nc.vector.memset(scale_table[64:128, :].bitcast(I32), 0)
+
+        bins = keep.tile([P, D], F32, name="bins")
+        nc.sync.dma_start(bins[:], bin_[0:1, :].rearrange("r (v d) -> (r v) d", d=D))
+
+        word_table = [keep.tile([P, T], U32, name="word_table%d" % o, align_bytes=64) for o in range(PASSES)]
+        w_raw = keep.tile([P, PASSES, 4 * M], F32, name="w_raw")
+        nc.sync.dma_start(word_table[0][:].bitcast(I32), x_words[0].rearrange("p c r -> p (c r)").bitcast(I32))
+        nc.sync.dma_start(w_raw[:], w1.rearrange("(o p j) m -> p o (j m)", o=PASSES, j=4))
+        nc.sync.dma_start(word_table[1][:].bitcast(I32), x_words[1].rearrange("p c r -> p (c r)").bitcast(I32))
+
+        ident = keep.tile([P, P], F32, name="ident")
+        make_identity(nc, ident[:])
+
+        def turn(dst, src, start=True, stop=True):
+            nc.tensor.matmul(dst, src, ident[:], start=start, stop=stop, is_transpose=True)
+
+        picked_scales = keep.tile([P, S], U8, name="picked_scales", align_bytes=64)
+        nc.vector.tensor_copy(picked_scales[:], scale_table[:].indirect(offsets[:]))
+        planes = keep.tile([P, S], U8, name="planes", align_bytes=64)
+        nc.vector.tensor_copy(planes[:].bitcast(I32), picked_scales[:].bitcast(I32))
+        for o in range(PASSES):
+            for q in range(4):
+                src, dst = 16 * o + 4 * q, 32 * q + 4 * o
+                if src != dst:
+                    nc.scalar.dma_start(planes[dst : dst + 4, :].bitcast(I32), picked_scales[src : src + 4, :].bitcast(I32))
+
+        bin_sum = keep.tile([P, 1], F32, name="bin_sum")
+        nc.vector.tensor_reduce(bin_sum[:], bins[:], AX.X, ALU.add)
+        bin_mean = keep.tile([P, 1], F32, name="bin_mean")
+        nc.vector.tensor_scalar(bin_mean[:], bin_sum[:], 1.0 / D, None, ALU.mult)
+        cen = keep.tile([P, D], F32, name="cen")
+        nc.vector.tensor_scalar(cen[:], bins[:], bin_mean[:], None, ALU.subtract)
+        cen_sq0 = keep.tile([P, D], F32, name="cen_sq0")
+        nc.vector.tensor_tensor(cen_sq0[:], cen[:], cen[:], ALU.mult)
+        cen_sq = keep.tile([P, D], F32, name="cen_sq")
+        nc.vector.tensor_scalar(cen_sq[:], cen_sq0[:], 0.05, None, ALU.add)
+        factor = [[psum.tile([P, DG, V], F32, name="factor%d%d" % (i, g)) for g in range(2)] for i in range(2)]
+        for i, col in enumerate((cen, cen_sq)):
+            for d in range(D):
+                turn(factor[i][d // DG][:, d % DG, :], col[:, d : d + 1].to_broadcast([P, P]))
+        result = psum.tile([P, V], F32, name="result")
+        turn(result[:], bin_mean[:, 0:1].to_broadcast([P, P]), start=True, stop=False)
+
+        w_grouped = keep.tile([P, PASSES, M, 4], BF16, name="w_grouped", align_bytes=64)
+        for o in range(PASSES):
+            nc.scalar.activation(w_grouped[:, o], w_raw[:, o, :].rearrange("p (j m) -> p m j", j=4), ACT.Copy)
+        w_codes = keep.tile([P, PASSES * M], U32, name="w_codes", align_bytes=64)
+        w_scales = keep.tile([P, PASSES * M], U8, name="w_scales", align_bytes=64)
+        nc.vector.quantize_mx(w_codes[:].bitcast(FP8X4), w_scales[:], w_grouped[:].rearrange("p o m j -> p (o m j)"))
+
+        picked0 = keep.tile([P, S], U32, name="picked0", align_bytes=64)
+        nc.vector.tensor_copy(picked0[:], word_table[0][:].indirect(offsets[:]))
+        picked1 = [keep.tile([P, HALF], U32, name="picked1_%d" % h, align_bytes=64) for h in range(2)]
+        for h in range(2):
+            nc.vector.tensor_copy(picked1[h][:], word_table[1][:].indirect(offsets[:, 32 * h : 32 * (h + 1)]))
+        y = [psum.tile([P, HALF], F32, name="y%d" % h, tag="bank%d" % h) for h in range(2)]
+        for o in range(PASSES):
+            for h in range(2):
+                cols = slice(h * HALF, (h + 1) * HALF)
+                words = picked0[:, cols] if o == 0 else picked1[h][:]
+                nc.tensor.matmul_mx(
+                    out=y[h][:],
+                    lhsT=w_codes[:, o * M : (o + 1) * M].bitcast(FP8X4),
+                    lhsT_scale=w_scales[:, o * M : (o + 1) * M],
+                    rhs=words.bitcast(FP8X4),
+                    rhs_scale=planes[4 * o : P, cols],
+                    start=(o == 0),
+                    stop=(o == PASSES - 1),
+                )
+
+        top = [keep.tile([P, VH], F32, name="top%d" % h) for h in range(2)]
+        for h in range(2):
+            nc.vector.tensor_reduce(top[h][:], y[h][:].rearrange("p (v d) -> p v d", d=D), AX.X, ALU.max)
+        z = [keep.tile([P, DG, V], F32, name="z%d" % g) for g in range(2)]
+        for g in range(2):
+            for h in range(2):
+                nc.vector.tensor_tensor(
+                    z[g][:, :, h * VH : (h + 1) * VH],
+                    y[h][:].rearrange("p (v d) -> p d v", d=D)[:, g * DG : (g + 1) * DG, :],
+                    top[h][:].unsqueeze(1).to_broadcast([P, DG, VH]),
+                    ALU.subtract,
+                )
+        ex = [keep.tile([P, DG, V], F32, name="ex%d" % g) for g in range(2)]
+        for g in range(2):
+            nc.scalar.activation(ex[g][:], z[g][:], ACT.Exp)
+
+        tot = psum.tile([P, M], F32, name="tot", tag="bank0")
+        sums = [psum.tile([P, M], F32, name="s1", tag="bank1"), psum.tile([P, M], F32, name="s2")]
+        weighted = [[keep.tile([P, DG, V], F32, name="weighted%d%d" % (i, g)) for g in range(2)] for i in range(2)]
+        for g in range(2):
+            for dd in range(DG):
+                turn(tot[:], ex[g][:, dd, :], start=(g == 0 and dd == 0), stop=(g == 1 and dd == DG - 1))
+            for i in range(2):
+                nc.vector.tensor_tensor(weighted[i][g][:], ex[g][:], factor[i][g][:], ALU.mult)
+                for dd in range(DG):
+                    turn(sums[i][:], weighted[i][g][:, dd, :], start=(g == 0 and dd == 0), stop=(g == 1 and dd == DG - 1))
+
+        tot_sb = keep.tile([P, M], F32, name="tot_sb")
+        nc.vector.tensor_copy(tot_sb[:], tot[:])
+        root = keep.tile([P, M], F32, name="root")
+        nc.scalar.activation(root[:], tot[:], ACT.Abs_reciprocal_sqrt)
+        s1_sq = keep.tile([P, M], F32, name="s1_sq")
+        nc.scalar.activation(s1_sq[:], sums[0][:], ACT.Square)
+        inv_tot = keep.tile([P, M], F32, name="inv_tot")
+        nc.scalar.activation(inv_tot[:], root[:], ACT.Square)
+        prod = keep.tile([P, M], F32, name="prod")
+        nc.vector.tensor_tensor(prod[:], sums[1][:], tot_sb[:], ALU.mult)
+        spread = keep.tile([P, M], F32, name="spread")
+        nc.vector.tensor_tensor(spread[:], prod[:], s1_sq[:], ALU.subtract)
+        inv_root = keep.tile([P, M], F32, name="inv_root")
+        nc.scalar.activation(inv_root[:], spread[:], ACT.Abs_reciprocal_sqrt, bias=1e-30)
+        mean_part = keep.tile([P, M], F32, name="mean_part")
+        nc.vector.tensor_tensor(mean_part[:], sums[0][:], inv_tot[:], ALU.mult)
+        half_spread = keep.tile([P, M], F32, name="half_spread")
+        nc.vector.scalar_tensor_tensor(half_spread[:], spread[:], 0.5, inv_tot[:], ALU.mult, ALU.mult)
+        dev_part = keep.tile([P, M], F32, name="dev_part")
+        nc.vector.tensor_tensor(dev_part[:], half_spread[:], inv_root[:], ALU.mult)
+        turn(result[:], mean_part[:], start=False, stop=False)
+        turn(result[:], dev_part[:], start=False, stop=True)
+        result_sb = keep.tile([P, V], F32, name="result_sb")
+        nc.vector.tensor_copy(result_sb[:], result[:])
+        nc.sync.dma_start(out, result_sb[:])

@@ -34,6 +34,9 @@ def tile_picked_ydfl_dist_p_kernel(tc, x_words, x_scales, w1, bin_, offs, out):
         offsets = keep.tile([P, S // 16], U16, name="offsets")
         nc.sync.dma_start(offsets[:], offs)
 
+        bins = keep.tile([P, D], F32, name="bins")
+        nc.sync.dma_start(bins[:], bin_[0:1, :].rearrange("r (v d) -> (r v) d", d=D))
+
         scale_table = keep.tile([P, T], U8, name="scale_table", align_bytes=64)
         nc.sync.dma_start(
             scale_table[0:32, :].bitcast(I32),
@@ -41,9 +44,6 @@ def tile_picked_ydfl_dist_p_kernel(tc, x_words, x_scales, w1, bin_, offs, out):
         )
         nc.vector.memset(scale_table[32:64, :].bitcast(I32), 0)
         nc.vector.memset(scale_table[64:128, :].bitcast(I32), 0)
-
-        bins = keep.tile([P, D], F32, name="bins")
-        nc.sync.dma_start(bins[:], bin_[0:1, :].rearrange("r (v d) -> (r v) d", d=D))
 
         word_table = [keep.tile([P, T], U32, name="word_table%d" % o, align_bytes=64) for o in range(PASSES)]
         w_raw = keep.tile([P, PASSES, 4 * M], F32, name="w_raw")
@@ -57,6 +57,17 @@ def tile_picked_ydfl_dist_p_kernel(tc, x_words, x_scales, w1, bin_, offs, out):
         def turn(dst, src, start=True, stop=True):
             nc.tensor.matmul(dst, src, ident[:], start=start, stop=stop, is_transpose=True)
 
+        bin_sum = keep.tile([P, 1], F32, name="bin_sum")
+        nc.vector.tensor_reduce(bin_sum[:], bins[:], AX.X, ALU.add)
+        neg_mean = keep.tile([P, 1], F32, name="neg_mean")
+        nc.vector.tensor_scalar(neg_mean[:], bin_sum[:], -1.0 / D, None, ALU.mult)
+        cen = keep.tile([P, D], F32, name="cen")
+        nc.scalar.activation(cen[:], bins[:], ACT.Identity, bias=neg_mean[:])
+        cen_sq0 = keep.tile([P, D], F32, name="cen_sq0")
+        nc.scalar.activation(cen_sq0[:], bins[:], ACT.Square, bias=neg_mean[:])
+        cen_sq = keep.tile([P, D], F32, name="cen_sq")
+        nc.scalar.activation(cen_sq[:], cen_sq0[:], ACT.Copy, bias=0.05)
+
         picked_scales = keep.tile([P, S], U8, name="picked_scales", align_bytes=64)
         nc.vector.tensor_copy(picked_scales[:], scale_table[:].indirect(offsets[:]))
         planes = keep.tile([P, S], U8, name="planes", align_bytes=64)
@@ -65,24 +76,18 @@ def tile_picked_ydfl_dist_p_kernel(tc, x_words, x_scales, w1, bin_, offs, out):
             for q in range(4):
                 src, dst = 16 * o + 4 * q, 32 * q + 4 * o
                 if src != dst:
-                    nc.scalar.dma_start(planes[dst : dst + 4, :].bitcast(I32), picked_scales[src : src + 4, :].bitcast(I32))
+                    queue = nc.gpsimd if (o, q) == (1, 3) else nc.scalar
+                    queue.dma_start(planes[dst : dst + 4, :].bitcast(I32), picked_scales[src : src + 4, :].bitcast(I32))
 
-        bin_sum = keep.tile([P, 1], F32, name="bin_sum")
-        nc.vector.tensor_reduce(bin_sum[:], bins[:], AX.X, ALU.add)
-        bin_mean = keep.tile([P, 1], F32, name="bin_mean")
-        nc.vector.tensor_scalar(bin_mean[:], bin_sum[:], 1.0 / D, None, ALU.mult)
-        cen = keep.tile([P, D], F32, name="cen")
-        nc.vector.tensor_scalar(cen[:], bins[:], bin_mean[:], None, ALU.subtract)
-        cen_sq0 = keep.tile([P, D], F32, name="cen_sq0")
-        nc.vector.tensor_tensor(cen_sq0[:], cen[:], cen[:], ALU.mult)
-        cen_sq = keep.tile([P, D], F32, name="cen_sq")
-        nc.vector.tensor_scalar(cen_sq[:], cen_sq0[:], 0.05, None, ALU.add)
         factor = [[psum.tile([P, DG, V], F32, name="factor%d%d" % (i, g)) for g in range(2)] for i in range(2)]
         for i, col in enumerate((cen, cen_sq)):
             for d in range(D):
                 turn(factor[i][d // DG][:, d % DG, :], col[:, d : d + 1].to_broadcast([P, P]))
-        result = psum.tile([P, V], F32, name="result")
-        turn(result[:], bin_mean[:, 0:1].to_broadcast([P, P]), start=True, stop=False)
+        sq_factor1 = keep.tile([P, VH, D], F32, name="sq_factor1")
+        for g in range(2):
+            nc.scalar.activation(sq_factor1[:, :, g * DG : (g + 1) * DG], factor[1][g][:, :, VH:V].rearrange("p d v -> p v d"), ACT.Copy)
+        mean_row = psum.tile([P, V], F32, name="mean_row")
+        turn(mean_row[:], neg_mean[:, 0:1].to_broadcast([P, P]))
 
         w_grouped = keep.tile([P, PASSES, M, 4], BF16, name="w_grouped", align_bytes=64)
         for o in range(PASSES):
@@ -111,55 +116,93 @@ def tile_picked_ydfl_dist_p_kernel(tc, x_words, x_scales, w1, bin_, offs, out):
                     stop=(o == PASSES - 1),
                 )
 
+        VQ = VH // 2
         top = [keep.tile([P, VH], F32, name="top%d" % h) for h in range(2)]
+        shapes = ([P, D, VH], [P, VH, D])
+        z = [keep.tile(shapes[h], F32, name="z%d" % h) for h in range(2)]
+        ex = [keep.tile(shapes[h], F32, name="ex%d" % h) for h in range(2)]
         for h in range(2):
-            nc.vector.tensor_reduce(top[h][:], y[h][:].rearrange("p (v d) -> p v d", d=D), AX.X, ALU.max)
-        z = [keep.tile([P, DG, V], F32, name="z%d" % g) for g in range(2)]
-        for g in range(2):
-            for h in range(2):
-                nc.vector.tensor_tensor(
-                    z[g][:, :, h * VH : (h + 1) * VH],
-                    y[h][:].rearrange("p (v d) -> p d v", d=D)[:, g * DG : (g + 1) * DG, :],
-                    top[h][:].unsqueeze(1).to_broadcast([P, DG, VH]),
-                    ALU.subtract,
-                )
-        ex = [keep.tile([P, DG, V], F32, name="ex%d" % g) for g in range(2)]
-        for g in range(2):
-            nc.scalar.activation(ex[g][:], z[g][:], ACT.Exp)
+            logits = y[h][:].rearrange("p (v d) -> p v d", d=D)
+            for u in range(2):
+                sides = slice(u * VQ, (u + 1) * VQ)
+                nc.vector.tensor_reduce(top[h][:, sides], logits[:, sides, :], AX.X, ALU.max)
+            for u in range(2):
+                sides = slice(u * VQ, (u + 1) * VQ)
+                if h == 0:
+                    nc.vector.tensor_tensor(
+                        z[h][:, :, sides],
+                        logits[:, sides, :].rearrange("p v d -> p d v"),
+                        top[h][:, sides].unsqueeze(1).to_broadcast([P, D, VQ]),
+                        ALU.subtract,
+                    )
+                else:
+                    nc.vector.tensor_tensor(
+                        z[h][:, sides, :], logits[:, sides, :], top[h][:, sides].unsqueeze(2).to_broadcast([P, VQ, D]), ALU.subtract
+                    )
+                    nc.scalar.activation(ex[h][:, sides, :], z[h][:, sides, :], ACT.Exp)
+            if h == 0:
+                nc.scalar.activation(ex[h][:], z[h][:], ACT.Exp)
 
-        tot = psum.tile([P, M], F32, name="tot", tag="bank0")
-        sums = [psum.tile([P, M], F32, name="s1", tag="bank1"), psum.tile([P, M], F32, name="s2")]
-        weighted = [[keep.tile([P, DG, V], F32, name="weighted%d%d" % (i, g)) for g in range(2)] for i in range(2)]
+        tot = keep.tile([P, V], F32, name="tot")
+        four0 = keep.tile([P, DG, VH], F32, name="four0")
+        nc.gpsimd.tensor_tensor(four0[:], ex[0][:, 0:DG, :], ex[0][:, DG:D, :], ALU.add)
+        weighted1 = [keep.tile([P, VH, D], F32, name="weighted1_%d" % i) for i in range(2)]
+        nc.gpsimd.tensor_tensor(weighted1[1][:], ex[1][:], sq_factor1[:], ALU.mult)
+        four1 = keep.tile([P, VH, DG], F32, name="four1")
+        nc.gpsimd.tensor_tensor(four1[:], weighted1[1][:, :, 0:DG], weighted1[1][:, :, DG:D], ALU.add)
+
+        weighted0 = [keep.tile([P, DG, 2, VH], F32, name="weighted0_%d" % g) for g in range(2)]
+        turned = psum.tile([P, M], F32, name="turned", tag="bank0")
         for g in range(2):
-            for dd in range(DG):
-                turn(tot[:], ex[g][:, dd, :], start=(g == 0 and dd == 0), stop=(g == 1 and dd == DG - 1))
             for i in range(2):
-                nc.vector.tensor_tensor(weighted[i][g][:], ex[g][:], factor[i][g][:], ALU.mult)
-                for dd in range(DG):
-                    turn(sums[i][:], weighted[i][g][:, dd, :], start=(g == 0 and dd == 0), stop=(g == 1 and dd == DG - 1))
+                nc.vector.tensor_tensor(weighted0[g][:, :, i, :], ex[0][:, g * DG : (g + 1) * DG, :], factor[i][g][:, :, 0:VH], ALU.mult)
+            for dd in range(DG):
+                turn(turned[:], weighted0[g][:, dd].rearrange("p i v -> p (i v)"), start=(g == 0 and dd == 0), stop=(g == 1 and dd == DG - 1))
+        for g in range(2):
+            nc.vector.tensor_tensor(
+                weighted1[0][:, :, g * DG : (g + 1) * DG],
+                ex[1][:, :, g * DG : (g + 1) * DG],
+                factor[0][g][:, :, VH:V].rearrange("p d v -> p v d"),
+                ALU.mult,
+            )
+        halves = (slice(0, VH), slice(VH, V))
+        root = keep.tile([P, V], F32, name="root")
+        inv_tot = keep.tile([P, V], F32, name="inv_tot")
+        nc.vector.tensor_reduce(tot[:, halves[0]], four0[:].rearrange("p d v -> p v d"), AX.X, ALU.add)
+        nc.scalar.activation(root[:, halves[0]], tot[:, halves[0]], ACT.Abs_reciprocal_sqrt)
+        nc.vector.tensor_reduce(tot[:, halves[1]], ex[1][:], AX.X, ALU.add)
+        turned_sb = keep.tile([P, M], F32, name="turned_sb")
+        nc.scalar.activation(turned_sb[:], turned[:], ACT.Copy)
+        sums0 = psum.tile([P, 2, VH], F32, name="sums0")
+        turn(sums0[:].rearrange("p i v -> p (i v)"), turned_sb[:])
+        nc.scalar.activation(root[:, halves[1]], tot[:, halves[1]], ACT.Abs_reciprocal_sqrt)
 
-        tot_sb = keep.tile([P, M], F32, name="tot_sb")
-        nc.vector.tensor_copy(tot_sb[:], tot[:])
-        root = keep.tile([P, M], F32, name="root")
-        nc.scalar.activation(root[:], tot[:], ACT.Abs_reciprocal_sqrt)
-        s1_sq = keep.tile([P, M], F32, name="s1_sq")
-        nc.scalar.activation(s1_sq[:], sums[0][:], ACT.Square)
-        inv_tot = keep.tile([P, M], F32, name="inv_tot")
+        sums1 = [keep.tile([P, VH], F32, name="sums1_%d" % i) for i in range(2)]
+        nc.vector.tensor_reduce(sums1[1][:], four1[:], AX.X, ALU.add)
+        nc.vector.tensor_reduce(sums1[0][:], weighted1[0][:], AX.X, ALU.add)
+
+        s1 = (sums0[:, 0, :], sums1[0][:])
+        s2 = (sums0[:, 1, :], sums1[1][:])
+        s1_sq = keep.tile([P, V], F32, name="s1_sq")
+        prod = keep.tile([P, V], F32, name="prod")
+        shift = keep.tile([P, V], F32, name="shift")
+        for h in range(2):
+            nc.scalar.activation(s1_sq[:, halves[h]], s1[h], ACT.Square)
         nc.scalar.activation(inv_tot[:], root[:], ACT.Square)
-        prod = keep.tile([P, M], F32, name="prod")
-        nc.vector.tensor_tensor(prod[:], sums[1][:], tot_sb[:], ALU.mult)
-        spread = keep.tile([P, M], F32, name="spread")
+        for h in (1, 0):
+            nc.vector.tensor_tensor(prod[:, halves[h]], s2[h], tot[:, halves[h]], ALU.mult)
+        spread = keep.tile([P, V], F32, name="spread")
         nc.vector.tensor_tensor(spread[:], prod[:], s1_sq[:], ALU.subtract)
-        inv_root = keep.tile([P, M], F32, name="inv_root")
+        inv_root = keep.tile([P, V], F32, name="inv_root")
         nc.scalar.activation(inv_root[:], spread[:], ACT.Abs_reciprocal_sqrt, bias=1e-30)
-        mean_part = keep.tile([P, M], F32, name="mean_part")
-        nc.vector.tensor_tensor(mean_part[:], sums[0][:], inv_tot[:], ALU.mult)
-        half_spread = keep.tile([P, M], F32, name="half_spread")
+        for h in range(2):
+            nc.vector.tensor_tensor(shift[:, halves[h]], s1[h], inv_tot[:, halves[h]], ALU.mult)
+        half_spread = keep.tile([P, V], F32, name="half_spread")
         nc.vector.scalar_tensor_tensor(half_spread[:], spread[:], 0.5, inv_tot[:], ALU.mult, ALU.mult)
-        dev_part = keep.tile([P, M], F32, name="dev_part")
+        mean_part = keep.tile([P, V], F32, name="mean_part")
+        nc.vector.tensor_tensor(mean_part[:], shift[:], mean_row[:], ALU.subtract)
+        dev_part = keep.tile([P, V], F32, name="dev_part")
         nc.vector.tensor_tensor(dev_part[:], half_spread[:], inv_root[:], ALU.mult)
-        turn(result[:], mean_part[:], start=False, stop=False)
-        turn(result[:], dev_part[:], start=False, stop=True)
-        result_sb = keep.tile([P, V], F32, name="result_sb")
-        nc.vector.tensor_copy(result_sb[:], result[:])
-        nc.sync.dma_start(out, result_sb[:])
+        result = keep.tile([P, V], F32, name="result")
+        nc.vector.tensor_tensor(result[:], dev_part[:], mean_part[:], ALU.add)
+        nc.sync.dma_start(out, result[:])

@@ -23,6 +23,7 @@ PASSES = 2
 HALF = S // 2
 VH = V // 2
 DG = D // 2
+PIVOT = D // 2
 
 
 def tile_picked_ydfl_dist_p_kernel(tc, x_words, x_scales, w1, bin_, offs, out):
@@ -34,8 +35,9 @@ def tile_picked_ydfl_dist_p_kernel(tc, x_words, x_scales, w1, bin_, offs, out):
         offsets = keep.tile([P, S // 16], U16, name="offsets")
         nc.sync.dma_start(offsets[:], offs)
 
-        bins = keep.tile([P, D], F32, name="bins")
-        nc.sync.dma_start(bins[:], bin_[0:1, :].rearrange("r (v d) -> (r v) d", d=D))
+        bins = keep.tile([P, 2, D], F32, name="bins")
+        for i in range(2):
+            nc.sync.dma_start(bins[i * VH : (i + 1) * VH], bin_[0].rearrange("(h v d) -> v h d", h=2, d=D))
 
         scale_table = keep.tile([P, T], U8, name="scale_table", align_bytes=64)
         nc.sync.dma_start(
@@ -57,16 +59,12 @@ def tile_picked_ydfl_dist_p_kernel(tc, x_words, x_scales, w1, bin_, offs, out):
         def turn(dst, src, start=True, stop=True):
             nc.tensor.matmul(dst, src, ident[:], start=start, stop=stop, is_transpose=True)
 
-        bin_sum = keep.tile([P, 1], F32, name="bin_sum")
-        nc.vector.tensor_reduce(bin_sum[:], bins[:], AX.X, ALU.add)
-        neg_mean = keep.tile([P, 1], F32, name="neg_mean")
-        nc.vector.tensor_scalar(neg_mean[:], bin_sum[:], -1.0 / D, None, ALU.mult)
-        cen = keep.tile([P, D], F32, name="cen")
-        nc.scalar.activation(cen[:], bins[:], ACT.Identity, bias=neg_mean[:])
-        cen_sq0 = keep.tile([P, D], F32, name="cen_sq0")
-        nc.scalar.activation(cen_sq0[:], bins[:], ACT.Square, bias=neg_mean[:])
-        cen_sq = keep.tile([P, D], F32, name="cen_sq")
-        nc.scalar.activation(cen_sq[:], cen_sq0[:], ACT.Copy, bias=0.05)
+        powers = keep.tile([P, 2, D], F32, name="powers")
+        squares = keep.tile([P, 2, D], F32, name="squares")
+        for h in range(2):
+            nc.scalar.activation(squares[VH:P, h], bins[VH:P, h], ACT.Square, scale=-1.0, bias=bins[VH:P, h, PIVOT : PIVOT + 1])
+        nc.gpsimd.tensor_tensor(powers[0:VH], bins[0:VH], bins[0:VH, :, PIVOT : PIVOT + 1].to_broadcast([VH, 2, D]), ALU.subtract)
+        nc.gpsimd.tensor_scalar(powers[VH:P], squares[VH:P], 0.05, None, ALU.add)
 
         picked_scales = keep.tile([P, S], U8, name="picked_scales", align_bytes=64)
         nc.vector.tensor_copy(picked_scales[:], scale_table[:].indirect(offsets[:]))
@@ -79,15 +77,16 @@ def tile_picked_ydfl_dist_p_kernel(tc, x_words, x_scales, w1, bin_, offs, out):
                     queue = nc.gpsimd if (o, q) == (1, 3) else nc.scalar
                     queue.dma_start(planes[dst : dst + 4, :].bitcast(I32), picked_scales[src : src + 4, :].bitcast(I32))
 
-        factor = [[psum.tile([P, DG, V], F32, name="factor%d%d" % (i, g)) for g in range(2)] for i in range(2)]
-        for i, col in enumerate((cen, cen_sq)):
+        factor = [[psum.tile([P, DG, 2, VH], F32, name="factor%d%d" % (h, g)) for g in range(2)] for h in range(2)]
+        for h in (1, 0):
             for d in range(D):
-                turn(factor[i][d // DG][:, d % DG, :], col[:, d : d + 1].to_broadcast([P, P]))
+                turn(factor[h][d // DG][:, d % DG].rearrange("p i v -> p (i v)"), powers[:, h, d : d + 1].to_broadcast([P, P]))
         sq_factor1 = keep.tile([P, VH, D], F32, name="sq_factor1")
         for g in range(2):
-            nc.scalar.activation(sq_factor1[:, :, g * DG : (g + 1) * DG], factor[1][g][:, :, VH:V].rearrange("p d v -> p v d"), ACT.Copy)
-        mean_row = psum.tile([P, V], F32, name="mean_row")
-        turn(mean_row[:], neg_mean[:, 0:1].to_broadcast([P, P]))
+            nc.scalar.activation(sq_factor1[:, :, g * DG : (g + 1) * DG], factor[1][g][:, :, 1, :].rearrange("p d v -> p v d"), ACT.Copy)
+        mean_rows = psum.tile([P, 2, P], F32, name="mean_rows")
+        for h in range(2):
+            turn(mean_rows[:, h, :], bins[:, h, PIVOT : PIVOT + 1].to_broadcast([P, P]))
 
         w_grouped = keep.tile([P, PASSES, M, 4], BF16, name="w_grouped", align_bytes=64)
         for o in range(PASSES):
@@ -135,14 +134,15 @@ def tile_picked_ydfl_dist_p_kernel(tc, x_words, x_scales, w1, bin_, offs, out):
                         top[h][:, sides].unsqueeze(1).to_broadcast([P, D, VQ]),
                         ALU.subtract,
                     )
+                    nc.scalar.activation(ex[h][:, :, sides], z[h][:, :, sides], ACT.Exp)
                 else:
                     nc.vector.tensor_tensor(
                         z[h][:, sides, :], logits[:, sides, :], top[h][:, sides].unsqueeze(2).to_broadcast([P, VQ, D]), ALU.subtract
                     )
                     nc.scalar.activation(ex[h][:, sides, :], z[h][:, sides, :], ACT.Exp)
-            if h == 0:
-                nc.scalar.activation(ex[h][:], z[h][:], ACT.Exp)
 
+        preload = keep.tile([P, 1], F32, name="preload")
+        nc.scalar.activation(preload[:], ex[1][:, VH - 1, D - 1 : D], ACT.Abs_reciprocal_sqrt)
         tot = keep.tile([P, V], F32, name="tot")
         four0 = keep.tile([P, DG, VH], F32, name="four0")
         nc.gpsimd.tensor_tensor(four0[:], ex[0][:, 0:DG, :], ex[0][:, DG:D, :], ALU.add)
@@ -154,15 +154,16 @@ def tile_picked_ydfl_dist_p_kernel(tc, x_words, x_scales, w1, bin_, offs, out):
         weighted0 = [keep.tile([P, DG, 2, VH], F32, name="weighted0_%d" % g) for g in range(2)]
         turned = psum.tile([P, M], F32, name="turned", tag="bank0")
         for g in range(2):
-            for i in range(2):
-                nc.vector.tensor_tensor(weighted0[g][:, :, i, :], ex[0][:, g * DG : (g + 1) * DG, :], factor[i][g][:, :, 0:VH], ALU.mult)
+            nc.vector.tensor_tensor(
+                weighted0[g][:], ex[0][:, g * DG : (g + 1) * DG, :].unsqueeze(2).to_broadcast([P, DG, 2, VH]), factor[0][g][:], ALU.mult
+            )
             for dd in range(DG):
                 turn(turned[:], weighted0[g][:, dd].rearrange("p i v -> p (i v)"), start=(g == 0 and dd == 0), stop=(g == 1 and dd == DG - 1))
         for g in range(2):
             nc.vector.tensor_tensor(
                 weighted1[0][:, :, g * DG : (g + 1) * DG],
                 ex[1][:, :, g * DG : (g + 1) * DG],
-                factor[0][g][:, :, VH:V].rearrange("p d v -> p v d"),
+                factor[1][g][:, :, 0, :].rearrange("p d v -> p v d"),
                 ALU.mult,
             )
         halves = (slice(0, VH), slice(VH, V))
@@ -200,7 +201,9 @@ def tile_picked_ydfl_dist_p_kernel(tc, x_words, x_scales, w1, bin_, offs, out):
         half_spread = keep.tile([P, V], F32, name="half_spread")
         nc.vector.scalar_tensor_tensor(half_spread[:], spread[:], 0.5, inv_tot[:], ALU.mult, ALU.mult)
         mean_part = keep.tile([P, V], F32, name="mean_part")
-        nc.vector.tensor_tensor(mean_part[:], shift[:], mean_row[:], ALU.subtract)
+        nc.vector.tensor_tensor(
+            mean_part[:].rearrange("p (h v) -> p h v", h=2), shift[:].rearrange("p (h v) -> p h v", h=2), mean_rows[:, :, 0:VH], ALU.add
+        )
         dev_part = keep.tile([P, V], F32, name="dev_part")
         nc.vector.tensor_tensor(dev_part[:], half_spread[:], inv_root[:], ALU.mult)
         result = keep.tile([P, V], F32, name="result")

@@ -77,13 +77,15 @@ def tile_picked_ydfl_dist_p_kernel(tc, x_words, x_scales, w1, bin_, offs, out):
                     queue = nc.gpsimd if (o, q) == (1, 3) else nc.scalar
                     queue.dma_start(planes[dst : dst + 4, :].bitcast(I32), picked_scales[src : src + 4, :].bitcast(I32))
 
-        factor = [[psum.tile([P, DG, 2, VH], F32, name="factor%d%d" % (h, g)) for g in range(2)] for h in range(2)]
+        factor = [[psum.tile([P, DG, 2, VH], F32, name="factor%d%d" % (h, g), tag="factor%d%d" % (h, g)) for g in range(2)] for h in range(2)]
         for h in (1, 0):
             for d in range(D):
                 turn(factor[h][d // DG][:, d % DG].rearrange("p i v -> p (i v)"), powers[:, h, d : d + 1].to_broadcast([P, P]))
         sq_factor1 = keep.tile([P, VH, D], F32, name="sq_factor1")
         for g in range(2):
             nc.scalar.activation(sq_factor1[:, :, g * DG : (g + 1) * DG], factor[1][g][:, :, 1, :].rearrange("p d v -> p v d"), ACT.Copy)
+        factor00 = keep.tile([P, DG, 2, VH], F32, name="factor00_sb")
+        nc.scalar.activation(factor00[:], factor[0][0][:], ACT.Copy)
         mean_rows = psum.tile([P, 2, P], F32, name="mean_rows")
         for h in range(2):
             turn(mean_rows[:, h, :], bins[:, h, PIVOT : PIVOT + 1].to_broadcast([P, P]))
@@ -101,8 +103,8 @@ def tile_picked_ydfl_dist_p_kernel(tc, x_words, x_scales, w1, bin_, offs, out):
         for h in range(2):
             nc.vector.tensor_copy(picked1[h][:], word_table[1][:].indirect(offsets[:, 32 * h : 32 * (h + 1)]))
         y = [psum.tile([P, HALF], F32, name="y%d" % h, tag="bank%d" % h) for h in range(2)]
-        for o in range(PASSES):
-            for h in range(2):
+        for h in range(2):
+            for o in range(PASSES):
                 cols = slice(h * HALF, (h + 1) * HALF)
                 words = picked0[:, cols] if o == 0 else picked1[h][:]
                 nc.tensor.matmul_mx(
@@ -141,24 +143,29 @@ def tile_picked_ydfl_dist_p_kernel(tc, x_words, x_scales, w1, bin_, offs, out):
                     )
                     nc.scalar.activation(ex[h][:, sides, :], z[h][:, sides, :], ACT.Exp)
 
+        tot = keep.tile([P, V], F32, name="tot")
+        tot_turned = psum.tile([P, M], F32, name="tot_turned", tag="bank0")
+        for t in range(DG):
+            turn(tot_turned[:], ex[0][:, 2 * t : 2 * t + 2, :].rearrange("p d v -> p (d v)"), start=(t == 0), stop=(t == DG - 1))
+        tot_turned_sb = keep.tile([P, M], F32, name="tot_turned_sb")
+        nc.scalar.activation(tot_turned_sb[:], tot_turned[:], ACT.Copy)
         preload = keep.tile([P, 1], F32, name="preload")
         nc.scalar.activation(preload[:], ex[1][:, VH - 1, D - 1 : D], ACT.Abs_reciprocal_sqrt)
-        tot = keep.tile([P, V], F32, name="tot")
-        four0 = keep.tile([P, DG, VH], F32, name="four0")
-        nc.gpsimd.tensor_tensor(four0[:], ex[0][:, 0:DG, :], ex[0][:, DG:D, :], ALU.add)
+
+        weighted0 = [keep.tile([P, DG, 2, VH], F32, name="weighted0_%d" % g) for g in range(2)]
+        turned = psum.tile([P, M], F32, name="turned", tag="bank1")
+        for g, (engine, source) in enumerate(((nc.gpsimd, factor00), (nc.vector, factor[0][1]))):
+            engine.tensor_tensor(
+                weighted0[g][:], ex[0][:, g * DG : (g + 1) * DG, :].unsqueeze(2).to_broadcast([P, DG, 2, VH]), source[:], ALU.mult
+            )
+            for dd in range(DG):
+                turn(turned[:], weighted0[g][:, dd].rearrange("p i v -> p (i v)"), start=(g == 0 and dd == 0), stop=(g == 1 and dd == DG - 1))
+        tot_pairs = psum.tile([P, 2, VH], F32, name="tot_pairs", tag="factor00")
+        turn(tot_pairs[:].rearrange("p d v -> p (d v)"), tot_turned_sb[:])
         weighted1 = [keep.tile([P, VH, D], F32, name="weighted1_%d" % i) for i in range(2)]
         nc.gpsimd.tensor_tensor(weighted1[1][:], ex[1][:], sq_factor1[:], ALU.mult)
         four1 = keep.tile([P, VH, DG], F32, name="four1")
         nc.gpsimd.tensor_tensor(four1[:], weighted1[1][:, :, 0:DG], weighted1[1][:, :, DG:D], ALU.add)
-
-        weighted0 = [keep.tile([P, DG, 2, VH], F32, name="weighted0_%d" % g) for g in range(2)]
-        turned = psum.tile([P, M], F32, name="turned", tag="bank0")
-        for g in range(2):
-            nc.vector.tensor_tensor(
-                weighted0[g][:], ex[0][:, g * DG : (g + 1) * DG, :].unsqueeze(2).to_broadcast([P, DG, 2, VH]), factor[0][g][:], ALU.mult
-            )
-            for dd in range(DG):
-                turn(turned[:], weighted0[g][:, dd].rearrange("p i v -> p (i v)"), start=(g == 0 and dd == 0), stop=(g == 1 and dd == DG - 1))
         for g in range(2):
             nc.vector.tensor_tensor(
                 weighted1[0][:, :, g * DG : (g + 1) * DG],
@@ -169,28 +176,27 @@ def tile_picked_ydfl_dist_p_kernel(tc, x_words, x_scales, w1, bin_, offs, out):
         halves = (slice(0, VH), slice(VH, V))
         root = keep.tile([P, V], F32, name="root")
         inv_tot = keep.tile([P, V], F32, name="inv_tot")
-        nc.vector.tensor_reduce(tot[:, halves[0]], four0[:].rearrange("p d v -> p v d"), AX.X, ALU.add)
-        nc.scalar.activation(root[:, halves[0]], tot[:, halves[0]], ACT.Abs_reciprocal_sqrt)
         nc.vector.tensor_reduce(tot[:, halves[1]], ex[1][:], AX.X, ALU.add)
         turned_sb = keep.tile([P, M], F32, name="turned_sb")
         nc.scalar.activation(turned_sb[:], turned[:], ACT.Copy)
         sums0 = psum.tile([P, 2, VH], F32, name="sums0")
         turn(sums0[:].rearrange("p i v -> p (i v)"), turned_sb[:])
-        nc.scalar.activation(root[:, halves[1]], tot[:, halves[1]], ACT.Abs_reciprocal_sqrt)
 
         sums1 = [keep.tile([P, VH], F32, name="sums1_%d" % i) for i in range(2)]
-        nc.vector.tensor_reduce(sums1[1][:], four1[:], AX.X, ALU.add)
         nc.vector.tensor_reduce(sums1[0][:], weighted1[0][:], AX.X, ALU.add)
+        nc.vector.tensor_reduce(tot[:, halves[0]], tot_pairs[:].rearrange("p d v -> p v d"), AX.X, ALU.add)
+        nc.scalar.activation(root[:], tot[:], ACT.Abs_reciprocal_sqrt)
+        nc.vector.tensor_reduce(sums1[1][:], four1[:], AX.X, ALU.add)
 
         s1 = (sums0[:, 0, :], sums1[0][:])
         s2 = (sums0[:, 1, :], sums1[1][:])
         s1_sq = keep.tile([P, V], F32, name="s1_sq")
         prod = keep.tile([P, V], F32, name="prod")
         shift = keep.tile([P, V], F32, name="shift")
-        for h in range(2):
+        for h in (1, 0):
             nc.scalar.activation(s1_sq[:, halves[h]], s1[h], ACT.Square)
         nc.scalar.activation(inv_tot[:], root[:], ACT.Square)
-        for h in (1, 0):
+        for h in range(2):
             nc.vector.tensor_tensor(prod[:, halves[h]], s2[h], tot[:, halves[h]], ALU.mult)
         spread = keep.tile([P, V], F32, name="spread")
         nc.vector.tensor_tensor(spread[:], prod[:], s1_sq[:], ALU.subtract)

from contextlib import ExitStack

import concourse.mybir as mybir
from concourse.masks import make_identity

K, T, S, D, M = 1024, 4096, 1024, 8, 128
V = S // D
FLOPS = 2 * K * M * S

F32 = mybir.dt.float32
BF16 = mybir.dt.bfloat16
I32 = mybir.dt.int32
U32 = mybir.dt.uint32
U16 = mybir.dt.uint16
U8 = mybir.dt.uint8
FP8X4 = mybir.dt.float8_e4m3fn_x4
ALU = mybir.AluOpType
ACT = mybir.ActivationFunctionType
AX = mybir.AxisListType

P = 128
PASSES = 2
HALF = S // 2
VH = V // 2
DG = D // 2
PIVOT = D // 2


def tile_picked_ydfl_dist_p_kernel(tc, x_words, x_scales, w1, bin_, offs, out):
    nc = tc.nc
    with ExitStack() as ctx:
        keep = ctx.enter_context(tc.tile_pool(name="keep", bufs=1))
        psum = ctx.enter_context(tc.psum_pool(name="psum", bufs=1))

        offsets = keep.tile([P, S // 16], U16, name="offsets")
        nc.sync.dma_start(offsets[:], offs)

        bins = keep.tile([P, 2, D], F32, name="bins")
        for i in range(2):
            nc.sync.dma_start(bins[i * VH : (i + 1) * VH], bin_[0].rearrange("(h v d) -> v h d", h=2, d=D))

        scale_table = keep.tile([P, T], U8, name="scale_table", align_bytes=64)
        nc.sync.dma_start(
            scale_table[0:32, :].bitcast(I32),
            x_scales.rearrange("o q c -> (o q) c").bitcast(I32),
        )
        nc.vector.memset(scale_table[32:64, :].bitcast(I32), 0)
        nc.vector.memset(scale_table[64:128, :].bitcast(I32), 0)

        word_table = [keep.tile([P, T], U32, name="word_table%d" % o, align_bytes=64) for o in range(PASSES)]
        w_raw = keep.tile([P, PASSES, 4 * M], F32, name="w_raw")
        nc.sync.dma_start(word_table[0][:].bitcast(I32), x_words[0].rearrange("p c r -> p (c r)").bitcast(I32))
        nc.sync.dma_start(w_raw[:], w1.rearrange("(o p j) m -> p o (j m)", o=PASSES, j=4))
        nc.sync.dma_start(word_table[1][:].bitcast(I32), x_words[1].rearrange("p c r -> p (c r)").bitcast(I32))

        ident = keep.tile([P, P], F32, name="ident")
        make_identity(nc, ident[:])

        def turn(dst, src, start=True, stop=True):
            nc.tensor.matmul(dst, src, ident[:], start=start, stop=stop, is_transpose=True)

        powers = keep.tile([P, 2, D], F32, name="powers")
        squares = keep.tile([P, 2, D], F32, name="squares")
        for h in range(2):
            nc.scalar.activation(squares[VH:P, h], bins[VH:P, h], ACT.Square, scale=-1.0, bias=bins[VH:P, h, PIVOT : PIVOT + 1])
        nc.gpsimd.tensor_tensor(powers[0:VH], bins[0:VH], bins[0:VH, :, PIVOT : PIVOT + 1].to_broadcast([VH, 2, D]), ALU.subtract)
        nc.gpsimd.tensor_scalar(powers[VH:P], squares[VH:P], 0.05, None, ALU.add)

        picked_scales = keep.tile([P, S], U8, name="picked_scales", align_bytes=64)
        nc.vector.tensor_copy(picked_scales[:], scale_table[:].indirect(offsets[:]))
        planes = keep.tile([P, S], U8, name="planes", align_bytes=64)
        nc.vector.tensor_copy(planes[:].bitcast(I32), picked_scales[:].bitcast(I32))
        for o in range(PASSES):
            for q in range(4):
                src, dst = 16 * o + 4 * q, 32 * q + 4 * o
                if src != dst:
                    queue = nc.gpsimd if (o, q) == (1, 3) else nc.scalar
                    queue.dma_start(planes[dst : dst + 4, :].bitcast(I32), picked_scales[src : src + 4, :].bitcast(I32))

        factor = [[psum.tile([P, DG, 2, VH], F32, name="factor%d%d" % (h, g), tag="factor%d%d" % (h, g)) for g in range(2)] for h in range(2)]
        for h in (1, 0):
            for d in range(D):
                turn(factor[h][d // DG][:, d % DG].rearrange("p i v -> p (i v)"), powers[:, h, d : d + 1].to_broadcast([P, P]))
        sq_factor1 = keep.tile([P, VH, D], F32, name="sq_factor1")
        for g in range(2):
            nc.scalar.activation(sq_factor1[:, :, g * DG : (g + 1) * DG], factor[1][g][:, :, 1, :].rearrange("p d v -> p v d"), ACT.Copy)
        factor00 = keep.tile([P, DG, 2, VH], F32, name="factor00_sb")
        nc.scalar.activation(factor00[:], factor[0][0][:], ACT.Copy)
        mean_rows = psum.tile([P, 2, P], F32, name="mean_rows")
        for h in range(2):
            turn(mean_rows[:, h, :], bins[:, h, PIVOT : PIVOT + 1].to_broadcast([P, P]))

        w_grouped = keep.tile([P, PASSES, M, 4], BF16, name="w_grouped", align_bytes=64)
        for o in range(PASSES):
            nc.scalar.activation(w_grouped[:, o], w_raw[:, o, :].rearrange("p (j m) -> p m j", j=4), ACT.Copy)
        w_codes = keep.tile([P, PASSES * M], U32, name="w_codes", align_bytes=64)
        w_scales = keep.tile([P, PASSES * M], U8, name="w_scales", align_bytes=64)
        nc.vector.quantize_mx(w_codes[:].bitcast(FP8X4), w_scales[:], w_grouped[:].rearrange("p o m j -> p (o m j)"))

        picked0 = keep.tile([P, S], U32, name="picked0", align_bytes=64)
        nc.vector.tensor_copy(picked0[:], word_table[0][:].indirect(offsets[:]))
        picked1 = [keep.tile([P, HALF], U32, name="picked1_%d" % h, align_bytes=64) for h in range(2)]
        for h in range(2):
            nc.vector.tensor_copy(picked1[h][:], word_table[1][:].indirect(offsets[:, 32 * h : 32 * (h + 1)]))
        y = [psum.tile([P, HALF], F32, name="y%d" % h, tag="bank%d" % h) for h in range(2)]
        for h in range(2):
            for o in range(PASSES):
                cols = slice(h * HALF, (h + 1) * HALF)
                words = picked0[:, cols] if o == 0 else picked1[h][:]
                nc.tensor.matmul_mx(
                    out=y[h][:],
                    lhsT=w_codes[:, o * M : (o + 1) * M].bitcast(FP8X4),
                    lhsT_scale=w_scales[:, o * M : (o + 1) * M],
                    rhs=words.bitcast(FP8X4),
                    rhs_scale=planes[4 * o : P, cols],
                    start=(o == 0),
                    stop=(o == PASSES - 1),
                )

        VQ = VH // 2
        top = [keep.tile([P, VH], F32, name="top%d" % h) for h in range(2)]
        shapes = ([P, D, VH], [P, VH, D])
        z = [keep.tile(shapes[h], F32, name="z%d" % h) for h in range(2)]
        ex = [keep.tile(shapes[h], F32, name="ex%d" % h) for h in range(2)]
        for h in range(2):
            logits = y[h][:].rearrange("p (v d) -> p v d", d=D)
            for u in range(2):
                sides = slice(u * VQ, (u + 1) * VQ)
                nc.vector.tensor_reduce(top[h][:, sides], logits[:, sides, :], AX.X, ALU.max)
            for u in range(2):
                sides = slice(u * VQ, (u + 1) * VQ)
                if h == 0:
                    nc.vector.tensor_tensor(
                        z[h][:, :, sides],
                        logits[:, sides, :].rearrange("p v d -> p d v"),
                        top[h][:, sides].unsqueeze(1).to_broadcast([P, D, VQ]),
                        ALU.subtract,
                    )
                    nc.scalar.activation(ex[h][:, :, sides], z[h][:, :, sides], ACT.Exp)
                else:
                    nc.vector.tensor_tensor(
                        z[h][:, sides, :], logits[:, sides, :], top[h][:, sides].unsqueeze(2).to_broadcast([P, VQ, D]), ALU.subtract
                    )
                    nc.scalar.activation(ex[h][:, sides, :], z[h][:, sides, :], ACT.Exp)

        tot = keep.tile([P, V], F32, name="tot")
        tot_turned = psum.tile([P, M], F32, name="tot_turned", tag="bank0")
        for t in range(DG):
            turn(tot_turned[:], ex[0][:, 2 * t : 2 * t + 2, :].rearrange("p d v -> p (d v)"), start=(t == 0), stop=(t == DG - 1))
        tot_turned_sb = keep.tile([P, M], F32, name="tot_turned_sb")
        nc.scalar.activation(tot_turned_sb[:], tot_turned[:], ACT.Copy)
        preload = keep.tile([P, 1], F32, name="preload")
        nc.scalar.activation(preload[:], ex[1][:, VH - 1, D - 1 : D], ACT.Abs_reciprocal_sqrt)

        weighted0 = [keep.tile([P, DG, 2, VH], F32, name="weighted0_%d" % g) for g in range(2)]
        turned = psum.tile([P, M], F32, name="turned", tag="bank1")
        for g, (engine, source) in enumerate(((nc.gpsimd, factor00), (nc.vector, factor[0][1]))):
            engine.tensor_tensor(
                weighted0[g][:], ex[0][:, g * DG : (g + 1) * DG, :].unsqueeze(2).to_broadcast([P, DG, 2, VH]), source[:], ALU.mult
            )
            for dd in range(DG):
                turn(turned[:], weighted0[g][:, dd].rearrange("p i v -> p (i v)"), start=(g == 0 and dd == 0), stop=(g == 1 and dd == DG - 1))
        tot_pairs = psum.tile([P, 2, VH], F32, name="tot_pairs", tag="factor00")
        turn(tot_pairs[:].rearrange("p d v -> p (d v)"), tot_turned_sb[:])
        weighted1 = [keep.tile([P, VH, D], F32, name="weighted1_%d" % i) for i in range(2)]
        nc.gpsimd.tensor_tensor(weighted1[1][:], ex[1][:], sq_factor1[:], ALU.mult)
        four1 = keep.tile([P, VH, DG], F32, name="four1")
        nc.gpsimd.tensor_tensor(four1[:], weighted1[1][:, :, 0:DG], weighted1[1][:, :, DG:D], ALU.add)
        for g in range(2):
            nc.vector.tensor_tensor(
                weighted1[0][:, :, g * DG : (g + 1) * DG],
                ex[1][:, :, g * DG : (g + 1) * DG],
                factor[1][g][:, :, 0, :].rearrange("p d v -> p v d"),
                ALU.mult,
            )
        halves = (slice(0, VH), slice(VH, V))
        root = keep.tile([P, V], F32, name="root")
        inv_tot = keep.tile([P, V], F32, name="inv_tot")
        nc.vector.tensor_reduce(tot[:, halves[1]], ex[1][:], AX.X, ALU.add)
        turned_sb = keep.tile([P, M], F32, name="turned_sb")
        nc.scalar.activation(turned_sb[:], turned[:], ACT.Copy)
        sums0 = psum.tile([P, 2, VH], F32, name="sums0")
        turn(sums0[:].rearrange("p i v -> p (i v)"), turned_sb[:])

        sums1 = [keep.tile([P, VH], F32, name="sums1_%d" % i) for i in range(2)]
        nc.vector.tensor_reduce(sums1[0][:], weighted1[0][:], AX.X, ALU.add)
        nc.vector.tensor_reduce(tot[:, halves[0]], tot_pairs[:].rearrange("p d v -> p v d"), AX.X, ALU.add)
        nc.scalar.activation(root[:], tot[:], ACT.Abs_reciprocal_sqrt)
        nc.vector.tensor_reduce(sums1[1][:], four1[:], AX.X, ALU.add)

        s1 = (sums0[:, 0, :], sums1[0][:])
        s2 = (sums0[:, 1, :], sums1[1][:])
        s1_sq = keep.tile([P, V], F32, name="s1_sq")
        prod = keep.tile([P, V], F32, name="prod")
        shift = keep.tile([P, V], F32, name="shift")
        for h in (1, 0):
            nc.scalar.activation(s1_sq[:, halves[h]], s1[h], ACT.Square)
        nc.scalar.activation(inv_tot[:], root[:], ACT.Square)
        for h in range(2):
            nc.vector.tensor_tensor(prod[:, halves[h]], s2[h], tot[:, halves[h]], ALU.mult)
        spread = keep.tile([P, V], F32, name="spread")
        nc.vector.tensor_tensor(spread[:], prod[:], s1_sq[:], ALU.subtract)
        inv_root = keep.tile([P, V], F32, name="inv_root")
        nc.scalar.activation(inv_root[:], spread[:], ACT.Abs_reciprocal_sqrt, bias=1e-30)
        for h in range(2):
            nc.vector.tensor_tensor(shift[:, halves[h]], s1[h], inv_tot[:, halves[h]], ALU.mult)
        half_spread = keep.tile([P, V], F32, name="half_spread")
        nc.vector.scalar_tensor_tensor(half_spread[:], spread[:], 0.5, inv_tot[:], ALU.mult, ALU.mult)
        mean_part = keep.tile([P, V], F32, name="mean_part")
        nc.vector.tensor_tensor(
            mean_part[:].rearrange("p (h v) -> p h v", h=2), shift[:].rearrange("p (h v) -> p h v", h=2), mean_rows[:, :, 0:VH], ALU.add
        )
        dev_part = keep.tile([P, V], F32, name="dev_part")
        nc.vector.tensor_tensor(dev_part[:], half_spread[:], inv_root[:], ALU.mult)
        result = keep.tile([P, V], F32, name="result")
        nc.vector.tensor_tensor(result[:], dev_part[:], mean_part[:], ALU.add)
        nc.sync.dma_start(out, result[:])
